import numpy as np
import ml_dtypes


def mxq(x, axis, fmt="e4m3"):
    dtype, down = {"e4m3": (ml_dtypes.float8_e4m3fn, 7), "e5m2": (ml_dtypes.float8_e5m2, 14)}[fmt]
    v = np.moveaxis(np.asarray(x, np.float32).astype(ml_dtypes.bfloat16).astype(np.float64), axis, -1)
    blocks = v.reshape(v.shape[:-1] + (-1, 32))
    amax = np.abs(blocks).max(-1, keepdims=True)
    byte = np.maximum(np.where(amax > 0, np.frexp(amax)[1] - 1 + 127, 0) - down, 1)
    scale = np.exp2(byte - 127.0)
    codes = (blocks / scale).astype(np.float32).astype(dtype).astype(np.float64)
    return np.moveaxis((codes * scale).reshape(v.shape), -1, axis)


WIDE = False


def mx_kscale(k):
    if not WIDE:
        return np.ones(k)
    levels = np.array([10, -10, 5, -5, 0])
    if k % 512:
        return np.exp2(np.random.permutation(np.resize(levels, k // 32))).repeat(32)
    a = np.empty((k // 512, 16))
    for p in range(k // 512):
        a[p, :8] = np.random.permutation(np.resize(levels, 8))
        for g in range(8):
            far = levels[np.abs(levels - a[p, g]) >= 10]
            a[p, g + 8] = far[np.random.randint(len(far))]
    return np.exp2(a.ravel()).repeat(32)


def f64(x):
    return np.asarray(x).astype(np.float64)


def striped(idx):
    return np.tile(idx.reshape(-1, 16).T, (8, 1)).astype(np.uint16)


def unstriped(offs):
    return offs[:16].T.reshape(-1).astype(np.int64)


E2M1 = np.array([0.0, 0.5, 1.0, 1.5, 2.0, 3.0, 4.0, 6.0, -0.0, -0.5, -1.0, -1.5, -2.0, -3.0, -4.0, -6.0])


def pack_weight(w, fmt):
    k, n = w.shape
    w = f64(np.asarray(w, np.float32).astype(ml_dtypes.bfloat16)).reshape(k // 32, 32, n)
    amax = np.abs(w).max(1)
    if fmt == "e4m3":
        byte = np.frexp(amax)[1] - 1 + 127 - 7
    else:
        mant, ex = np.frexp(amax / 6.0)
        byte = np.where(mant > 0.5, ex, ex - 1) + 127
    byte = np.clip(np.where(amax > 0, byte, 1), 1, 254)
    scaled = (w * np.exp2(127.0 - byte)[:, None, :]).reshape(k, n).astype(np.float32)
    by_word = np.ascontiguousarray(scaled.reshape(k // 512, 128, 4, n).transpose(0, 1, 3, 2))
    if fmt == "e4m3":
        words = by_word.astype(ml_dtypes.float8_e4m3fn).view(np.uint8)
    else:
        c = by_word.astype(ml_dtypes.float4_e2m1fn).view(np.uint8) & 0xF
        words = (c[..., 0::2] | (c[..., 1::2] << 4)).reshape(k // 512, 128, 2 * n)
    return np.ascontiguousarray(words), np.ascontiguousarray(byte.astype(np.uint8).reshape(k // 512, 16, n))


def unpack_weight(words, scales, fmt):
    g, _, n = scales.shape
    words = np.ascontiguousarray(words).reshape(g, 128, n, -1)
    if fmt == "e4m3":
        vals = words.view(ml_dtypes.float8_e4m3fn).astype(np.float64)
    else:
        nib = np.empty((g, 128, n, 4), np.uint8)
        nib[..., 0::2] = words & 0xF
        nib[..., 1::2] = words >> 4
        vals = E2M1[nib]
    vals = vals * np.repeat(np.exp2(scales.astype(np.float64) - 127.0), 8, axis=1)[..., None]
    return vals.transpose(0, 1, 3, 2).reshape(g * 512, n)


def relu(v):
    return np.maximum(v, 0.0)


K, T, E, C, N = 2048, 1024, 16, 256, 128
TOP = 4


def by_expert(wq, xq):
    return np.concatenate([wq[e].T @ xq[:, e * C:(e + 1) * C] for e in range(E)], axis=1)


def setup_inputs():
    n = np.random.standard_normal
    s = mx_kscale(K)[:, None]
    deal = np.repeat(np.arange(E), C).reshape(TOP, T)[:, np.random.permutation(T)]
    deal = np.take_along_axis(deal, np.argsort(np.random.rand(TOP, T), axis=0), axis=0)
    for _ in range(8):
        s_, t_ = np.random.permutation(T).reshape(2, -1); r = np.random.randint(TOP, size=T // 2); x, y = deal[r, s_].copy(), deal[r, t_].copy()
        ok = ~((deal[:, s_] == y).any(0) | (deal[:, t_] == x).any(0)); deal[r[ok], s_[ok]] = y[ok]; deal[r[ok], t_[ok]] = x[ok]
    order = np.lexsort((np.random.rand(TOP * T), deal.reshape(-1)))
    slot_token = order % T; pos = np.empty(TOP * T, np.int64); pos[order] = np.arange(TOP * T); pos = pos.reshape(TOP, T)
    g = np.random.uniform(0.5, 1.5, (TOP, T)); g = g / g.sum(0)
    x = pack_weight(n((K, T)) * s, "e4m3")
    return {
        "x_words": x[0],
        "x_scales": x[1],
        "w": (n((E + 1, K, N)) / np.sqrt(K) / s[None]).astype(np.float32),
        "b": (0.3 * n((N, E + 1))).astype(np.float32),
        "gate": np.stack([np.tile(r, (N, 1)) for r in g]).astype(np.float32),
        "offs": striped(slot_token),
        "pos1": striped(pos[0]),
        "pos2": striped(pos[1]),
        "pos3": striped(pos[2]),
        "pos4": striped(pos[3]),
    }


def reference(x_words, x_scales, w, b, gate, offs, pos1, pos2, pos3, pos4):
    idx = unstriped(offs)
    wq = mxq(f64(w), 1, "e4m3")
    xs = unpack_weight(x_words, x_scales, "e4m3")
    ys = relu((wq[E].T @ xs) + f64(b)[:, E:])
    xq = unpack_weight(x_words, x_scales, "e4m3")[:, idx]
    y = by_expert(wq, xq)
    y = relu(y + np.repeat(f64(b)[:, :E], C, axis=1))
    return ys + sum(f64(gate[r]) * y[:, unstriped(p)] for r, p in enumerate((pos1, pos2, pos3, pos4)))

@@ -1,0 +1,210 @@
+from contextlib import ExitStack
+
+import concourse.mybir as mybir
+
+K, T, E, C, N = 2048, 1024, 16, 256, 128
+TOP = 4
+S = E * C
+FLOPS = 2 * K * N * (S + T)
+
+F32 = mybir.dt.float32
+BF16 = mybir.dt.bfloat16
+I32 = mybir.dt.int32
+U32 = mybir.dt.uint32
+U16 = mybir.dt.uint16
+U8 = mybir.dt.uint8
+FP8X4 = mybir.dt.float8_e4m3fn_x4
+MULT = mybir.AluOpType.mult
+ADD = mybir.AluOpType.add
+RELU = mybir.ActivationFunctionType.Relu
+
+P = 128
+PACK = 4
+PASSES = K // (P * PACK)
+PER_COL = 16
+PAIR = 2 * C
+BANK = 512
+RAW_BUFS = 6
+
+
+def tile_moe_shr_lin_relu_kernel(
+    tc, x_words, x_scales, w, b, gate, offs, pos1, pos2, pos3, pos4, out
+):
+    nc = tc.nc
+    with ExitStack() as ctx:
+        keep = ctx.enter_context(tc.tile_pool(name="keep", bufs=1))
+        stream = ctx.enter_context(tc.tile_pool(name="stream", bufs=RAW_BUFS))
+        rounded = ctx.enter_context(tc.tile_pool(name="rounded", bufs=3))
+        picked = ctx.enter_context(tc.tile_pool(name="picked", bufs=8))
+        psum = ctx.enter_context(tc.psum_pool(name="psum", bufs=6))
+        psum_shared = ctx.enter_context(tc.psum_pool(name="psum_shared", bufs=2))
+
+        slot_tokens = keep.tile([P, S // PER_COL], U16, name="slot_tokens")
+        nc.sync.dma_start(slot_tokens[:], offs)
+
+        tok_scales = keep.tile([P, T], U8, name="tok_scales", align_bytes=64)
+        nc.vector.memset(tok_scales[:].bitcast(I32), 0)
+        for q in range(4):
+            nc.scalar.dma_start(
+                tok_scales[32 * q : 32 * q + 16, :].bitcast(I32),
+                x_scales[:, 4 * q : 4 * q + 4, :].bitcast(I32),
+            )
+
+        tok_words = [keep.tile([P, T], I32, name="tok_words%d" % a, align_bytes=64) for a in range(PASSES)]
+        raw = {}
+
+        def load_words(a):
+            nc.sync.dma_start(tok_words[a][:], x_words[a].rearrange("p t r -> p (t r)").bitcast(I32))
+
+        def load_weight(e):
+            raw[e] = stream.tile([P, PASSES, PACK * N], F32, name="raw")
+            nc.sync.dma_start(raw[e][:], w[e].rearrange("(a p j) n -> p a (j n)", a=PASSES, j=PACK))
+
+        bias = keep.tile([P, E + 1], F32, name="bias")
+        load_weight(0)
+        load_weight(1)
+        load_words(0)
+        load_words(1)
+        load_weight(2)
+        load_words(2)
+        load_weight(3)
+        load_words(3)
+        nc.sync.dma_start(bias[:], b)
+        load_weight(4)
+        load_weight(5)
+        token_slots = []
+        for r, pos in enumerate((pos1, pos2, pos3, pos4)):
+            token_slots.append(keep.tile([P, T // PER_COL], U16, name="token_slots%d" % r))
+            nc.sync.dma_start(token_slots[r][:], pos)
+
+        grouped = {}
+
+        def round_weight(e):
+            grouped[e] = rounded.tile([P, PASSES, N * PACK], BF16, name="grouped", align_bytes=64)
+            nc.scalar.copy(
+                grouped[e][:].rearrange("p a (c i j) -> p a c j i", i=4, j=PACK),
+                raw[e][:].rearrange("p a (j c i) -> p a c j i", i=4, j=PACK),
+            )
+            if e + RAW_BUFS <= E:
+                load_weight(e + RAW_BUFS)
+
+        w_words = keep.tile([P, E + 1, PASSES * N], U32, name="w_words", align_bytes=64)
+        w_scales = keep.tile([P, E + 1, PASSES * N], U8, name="w_scales", align_bytes=64)
+
+        def quantize_weight(e):
+            nc.vector.quantize_mx(
+                out=w_words[:, e, :].bitcast(FP8X4),
+                scales=w_scales[:, e, :],
+                in_=grouped[e][:].rearrange("p a x -> p (a x)"),
+            )
+
+        def multiply(acc, e, a, words, scales):
+            nc.tensor.matmul_mx(
+                out=acc,
+                lhsT=w_words[:, e, a * N : (a + 1) * N].bitcast(FP8X4),
+                lhsT_scale=w_scales[:, e, a * N : (a + 1) * N],
+                rhs=words.bitcast(FP8X4),
+                rhs_scale=scales,
+                start=(a == 0),
+                stop=(a == PASSES - 1),
+            )
+
+        def entries(lst, first, count):
+            return lst[:, first // PER_COL : (first + count) // PER_COL]
+
+        slot_scales = keep.tile([P, S], U8, name="slot_scales", align_bytes=64)
+        round_weight(0)
+        round_weight(1)
+        for g in range(E // 2):
+            nc.vector.tensor_copy(
+                slot_scales[:, g * PAIR : (g + 1) * PAIR],
+                tok_scales[:].indirect(entries(slot_tokens, g * PAIR, PAIR)),
+            )
+
+        y = keep.tile([P, S], F32, name="y")
+        gates = []
+
+        def gather_words(dst, a, first, count):
+            nc.vector.tensor_copy(dst, tok_words[a][:].bitcast(U32).indirect(entries(slot_tokens, first, count)))
+
+        def activate(dst, acc, e):
+            nc.scalar.activation(dst, acc, RELU, bias=bias[:, e : e + 1])
+
+        pending = []
+        for g in range(E // 2):
+            last = g == E // 2 - 1
+            round_weight(2 * g + 2)
+            if not last:
+                round_weight(2 * g + 3)
+            if 2 * g + 3 + RAW_BUFS == E + 1:
+                for h in range(2):
+                    gates.append(stream.tile([P, 2, T], F32, name="raw"))
+                    nc.sync.dma_start(gates[h][:], gate[2 * h : 2 * h + 2].rearrange("r p t -> p r t"))
+            words = [picked.tile([P, PAIR], U32, name="slot_words", align_bytes=64) for a in range(PASSES)]
+            gather_words(words[0][:], 0, g * PAIR, PAIR)
+            quantize_weight(2 * g)
+            gather_words(words[1][:], 1, g * PAIR, PAIR)
+            gather_words(words[2][:], 2, g * PAIR, PAIR)
+            quantize_weight(2 * g + 1)
+            if last:
+                gather_words(words[3][:, 0:C], 3, g * PAIR, C)
+                gather_words(words[3][:, C:PAIR], 3, g * PAIR + C, C)
+            else:
+                gather_words(words[3][:], 3, g * PAIR, PAIR)
+            for dst, acc, e in pending:
+                activate(dst, acc, e)
+            pending = []
+            accs = [psum.tile([P, C], F32, name="acc") for u in range(2)]
+            for a in range(PASSES):
+                for u in range(2):
+                    e = 2 * g + u
+                    multiply(
+                        accs[u][:], e, a,
+                        words[a][:, u * C : (u + 1) * C],
+                        slot_scales[4 * a : P, e * C : (e + 1) * C],
+                    )
+            for u in range(2):
+                e = 2 * g + u
+                pending.append((y[:, e * C : (e + 1) * C], accs[u][:], e))
+        for dst, acc, e in pending:
+            activate(dst, acc, e)
+
+        quantize_weight(E)
+        ys = keep.tile([P, T], F32, name="ys")
+        for h in range(T // BANK):
+            cols = slice(h * BANK, (h + 1) * BANK)
+            acc = psum_shared.tile([P, BANK], F32, name="acc_shared")
+            for a in range(PASSES):
+                multiply(acc[:], E, a, tok_words[a][:, cols], tok_scales[4 * a : P, cols])
+            activate(ys[:, cols], acc[:], E)
+
+        terms = keep.tile([P, TOP, T], F32, name="terms")
+        result = keep.tile([P, T], F32, name="result")
+
+        def fetch(r, first, count):
+            nc.vector.tensor_tensor(
+                terms[:, r, first : first + count],
+                y[:].indirect(entries(token_slots[r], first, count)),
+                gates[r // 2][:, r % 2, first : first + count],
+                MULT,
+            )
+
+        def add(dst, lhs, rhs):
+            nc.vector.tensor_tensor(dst, lhs, rhs, ADD)
+
+        finish = None
+        for first, count in ((0, 640), (640, 384)):
+            cols = slice(first, first + count)
+            fetch(0, first, count)
+            if finish is not None:
+                add(result[:, finish], terms[:, 0, finish], terms[:, 2, finish])
+                nc.sync.dma_start(out[:, finish], result[:, finish])
+            fetch(1, first, count)
+            fetch(2, first, count)
+            add(terms[:, 0, cols], terms[:, 0, cols], terms[:, 1, cols])
+            fetch(3, first, count)
+            add(terms[:, 2, cols], terms[:, 2, cols], ys[:, cols])
+            add(terms[:, 0, cols], terms[:, 0, cols], terms[:, 3, cols])
+            finish = cols
+        add(result[:, finish], terms[:, 0, finish], terms[:, 2, finish])
+        nc.sync.dma_start(out[:, finish], result[:, finish])

@@ -24,7 +24,7 @@ PASSES = K // (P * PACK)
 PER_COL = 16
 PAIR = 2 * C
 BANK = 512
-RAW_BUFS = 6
+BIAS_BAY = 13
 
 
 def tile_moe_shr_lin_relu_kernel(
@@ -33,11 +33,13 @@ def tile_moe_shr_lin_relu_kernel(
     nc = tc.nc
     with ExitStack() as ctx:
         keep = ctx.enter_context(tc.tile_pool(name="keep", bufs=1))
-        stream = ctx.enter_context(tc.tile_pool(name="stream", bufs=RAW_BUFS))
-        rounded = ctx.enter_context(tc.tile_pool(name="rounded", bufs=3))
-        picked = ctx.enter_context(tc.tile_pool(name="picked", bufs=8))
-        psum = ctx.enter_context(tc.psum_pool(name="psum", bufs=6))
-        psum_shared = ctx.enter_context(tc.psum_pool(name="psum_shared", bufs=2))
+        bays = ctx.enter_context(tc.tile_pool(name="bays", bufs=1))
+        rounded = ctx.enter_context(tc.tile_pool(name="rounded", bufs=5))
+        packed = ctx.enter_context(tc.tile_pool(name="packed", bufs=10))
+        psum = ctx.enter_context(tc.psum_pool(name="psum", bufs=8))
+
+        def in_bay(e, shape, dtype, name):
+            return bays.tile(shape, dtype, name=name, tag="bay%d" % e, align_bytes=64)
 
         slot_tokens = keep.tile([P, S // PER_COL], U16, name="slot_tokens")
         nc.sync.dma_start(slot_tokens[:], offs)
@@ -45,7 +47,7 @@ def tile_moe_shr_lin_relu_kernel(
         tok_scales = keep.tile([P, T], U8, name="tok_scales", align_bytes=64)
         nc.vector.memset(tok_scales[:].bitcast(I32), 0)
         for q in range(4):
-            nc.scalar.dma_start(
+            nc.sync.dma_start(
                 tok_scales[32 * q : 32 * q + 16, :].bitcast(I32),
                 x_scales[:, 4 * q : 4 * q + 4, :].bitcast(I32),
             )
@@ -57,27 +59,35 @@ def tile_moe_shr_lin_relu_kernel(
             nc.sync.dma_start(tok_words[a][:], x_words[a].rearrange("p t r -> p (t r)").bitcast(I32))
 
         def load_weight(e):
-            raw[e] = stream.tile([P, PASSES, PACK * N], F32, name="raw")
+            raw[e] = in_bay(e, [P, PASSES, PACK * N], F32, "raw%d" % e)
             nc.sync.dma_start(raw[e][:], w[e].rearrange("(a p j) n -> p a (j n)", a=PASSES, j=PACK))
 
-        bias = keep.tile([P, E + 1], F32, name="bias")
         load_weight(0)
         load_weight(1)
         load_words(0)
-        load_words(1)
         load_weight(2)
+        load_words(1)
         load_words(2)
         load_weight(3)
         load_words(3)
-        nc.sync.dma_start(bias[:], b)
-        load_weight(4)
-        load_weight(5)
+        for e in range(4, E + 1):
+            load_weight(e)
         token_slots = []
         for r, pos in enumerate((pos1, pos2, pos3, pos4)):
             token_slots.append(keep.tile([P, T // PER_COL], U16, name="token_slots%d" % r))
             nc.sync.dma_start(token_slots[r][:], pos)
 
-        grouped = {}
+        def entries(lst, first, count):
+            return lst[:, first // PER_COL : (first + count) // PER_COL]
+
+        slot_scales = keep.tile([P, S], U8, name="slot_scales", align_bytes=64)
+        for g in range(E // 2):
+            nc.vector.tensor_copy(
+                slot_scales[:, g * PAIR : (g + 1) * PAIR],
+                tok_scales[:].indirect(entries(slot_tokens, g * PAIR, PAIR)),
+            )
+
+        grouped, w_words, w_scales = {}, {}, {}
 
         def round_weight(e):
             grouped[e] = rounded.tile([P, PASSES, N * PACK], BF16, name="grouped", align_bytes=64)
@@ -85,105 +95,94 @@ def tile_moe_shr_lin_relu_kernel(
                 grouped[e][:].rearrange("p a (c i j) -> p a c j i", i=4, j=PACK),
                 raw[e][:].rearrange("p a (j c i) -> p a c j i", i=4, j=PACK),
             )
-            if e + RAW_BUFS <= E:
-                load_weight(e + RAW_BUFS)
-
-        w_words = keep.tile([P, E + 1, PASSES * N], U32, name="w_words", align_bytes=64)
-        w_scales = keep.tile([P, E + 1, PASSES * N], U8, name="w_scales", align_bytes=64)
 
         def quantize_weight(e):
+            w_words[e] = packed.tile([P, PASSES * N], U32, name="w_words", align_bytes=64)
+            w_scales[e] = packed.tile([P, PASSES * N], U8, name="w_scales", align_bytes=64)
             nc.vector.quantize_mx(
-                out=w_words[:, e, :].bitcast(FP8X4),
-                scales=w_scales[:, e, :],
+                out=w_words[e][:].bitcast(FP8X4),
+                scales=w_scales[e][:],
                 in_=grouped[e][:].rearrange("p a x -> p (a x)"),
             )
 
         def multiply(acc, e, a, words, scales):
             nc.tensor.matmul_mx(
                 out=acc,
-                lhsT=w_words[:, e, a * N : (a + 1) * N].bitcast(FP8X4),
-                lhsT_scale=w_scales[:, e, a * N : (a + 1) * N],
+                lhsT=w_words[e][:, a * N : (a + 1) * N].bitcast(FP8X4),
+                lhsT_scale=w_scales[e][:, a * N : (a + 1) * N],
                 rhs=words.bitcast(FP8X4),
                 rhs_scale=scales,
                 start=(a == 0),
                 stop=(a == PASSES - 1),
             )
 
-        def entries(lst, first, count):
-            return lst[:, first // PER_COL : (first + count) // PER_COL]
-
-        slot_scales = keep.tile([P, S], U8, name="slot_scales", align_bytes=64)
-        round_weight(0)
-        round_weight(1)
-        for g in range(E // 2):
-            nc.vector.tensor_copy(
-                slot_scales[:, g * PAIR : (g + 1) * PAIR],
-                tok_scales[:].indirect(entries(slot_tokens, g * PAIR, PAIR)),
-            )
-
-        y = keep.tile([P, S], F32, name="y")
-        gates = []
-
         def gather_words(dst, a, first, count):
             nc.vector.tensor_copy(dst, tok_words[a][:].bitcast(U32).indirect(entries(slot_tokens, first, count)))
+
+        slot_words = {}
+
+        def gather_passes(e):
+            g, u = divmod(e, 2)
+            if e == BIAS_BAY:
+                return
+            passes = range(PASSES) if e == BIAS_BAY - 1 else range(2 * u, 2 * u + 2)
+            held = in_bay(e, [P, len(passes), PAIR], U32, "slot_words%d" % e)
+            for i, a in enumerate(passes):
+                slot_words[g, a] = held[:, i, :]
+                if e == E - 1 and a == PASSES - 1:
+                    gather_words(held[:, i, 0:C], a, g * PAIR, C)
+                    gather_words(held[:, i, C:PAIR], a, g * PAIR + C, C)
+                else:
+                    gather_words(held[:, i, :], a, g * PAIR, PAIR)
+
+        for e in range(E):
+            round_weight(e)
+            quantize_weight(e)
+            gather_passes(e)
+        round_weight(E)
+
+        bias = in_bay(BIAS_BAY, [P, E + 1], F32, "bias")
+        nc.sync.dma_start(bias[:], b)
 
         def activate(dst, acc, e):
             nc.scalar.activation(dst, acc, RELU, bias=bias[:, e : e + 1])
 
-        pending = []
+        y = keep.tile([P, S], F32, name="y")
         for g in range(E // 2):
-            last = g == E // 2 - 1
-            round_weight(2 * g + 2)
-            if not last:
-                round_weight(2 * g + 3)
-            if 2 * g + 3 + RAW_BUFS == E + 1:
-                for h in range(2):
-                    gates.append(stream.tile([P, 2, T], F32, name="raw"))
-                    nc.sync.dma_start(gates[h][:], gate[2 * h : 2 * h + 2].rearrange("r p t -> p r t"))
-            words = [picked.tile([P, PAIR], U32, name="slot_words", align_bytes=64) for a in range(PASSES)]
-            gather_words(words[0][:], 0, g * PAIR, PAIR)
-            quantize_weight(2 * g)
-            gather_words(words[1][:], 1, g * PAIR, PAIR)
-            gather_words(words[2][:], 2, g * PAIR, PAIR)
-            quantize_weight(2 * g + 1)
-            if last:
-                gather_words(words[3][:, 0:C], 3, g * PAIR, C)
-                gather_words(words[3][:, C:PAIR], 3, g * PAIR + C, C)
-            else:
-                gather_words(words[3][:], 3, g * PAIR, PAIR)
-            for dst, acc, e in pending:
-                activate(dst, acc, e)
-            pending = []
-            accs = [psum.tile([P, C], F32, name="acc") for u in range(2)]
+            accs = [psum.tile([P, BANK], F32, name="acc") for u in range(2)]
             for a in range(PASSES):
                 for u in range(2):
                     e = 2 * g + u
                     multiply(
-                        accs[u][:], e, a,
-                        words[a][:, u * C : (u + 1) * C],
+                        accs[u][:, 0:C], e, a,
+                        slot_words[g, a][:, u * C : (u + 1) * C],
                         slot_scales[4 * a : P, e * C : (e + 1) * C],
                     )
             for u in range(2):
                 e = 2 * g + u
-                pending.append((y[:, e * C : (e + 1) * C], accs[u][:], e))
-        for dst, acc, e in pending:
-            activate(dst, acc, e)
+                activate(y[:, e * C : (e + 1) * C], accs[u][:, 0:C], e)
+
+        gates = []
+        for h in range(2):
+            gates.append(in_bay(h, [P, 2, T], F32, "gates%d" % h))
+            nc.sync.dma_start(gates[h][:], gate[2 * h : 2 * h + 2].rearrange("r p t -> p r t"))
 
         quantize_weight(E)
-        ys = keep.tile([P, T], F32, name="ys")
+        ys = in_bay(4, [P, T], F32, "ys")
         for h in range(T // BANK):
             cols = slice(h * BANK, (h + 1) * BANK)
-            acc = psum_shared.tile([P, BANK], F32, name="acc_shared")
+            acc = psum.tile([P, BANK], F32, name="acc")
             for a in range(PASSES):
                 multiply(acc[:], E, a, tok_words[a][:, cols], tok_scales[4 * a : P, cols])
             activate(ys[:, cols], acc[:], E)
 
-        terms = keep.tile([P, TOP, T], F32, name="terms")
-        result = keep.tile([P, T], F32, name="result")
+        halves = [in_bay(2 + h, [P, 2, T], F32, "terms%d" % h) for h in range(2)]
+        terms = [halves[r // 2][:, r % 2, :] for r in range(TOP)]
+        result = in_bay(5, [P, T], F32, "result")
 
         def fetch(r, first, count):
             nc.vector.tensor_tensor(
-                terms[:, r, first : first + count],
+                terms[r][:, first : first + count],
                 y[:].indirect(entries(token_slots[r], first, count)),
                 gates[r // 2][:, r % 2, first : first + count],
                 MULT,
@@ -197,14 +196,14 @@ def tile_moe_shr_lin_relu_kernel(
             cols = slice(first, first + count)
             fetch(0, first, count)
             if finish is not None:
-                add(result[:, finish], terms[:, 0, finish], terms[:, 2, finish])
+                add(result[:, finish], terms[0][:, finish], terms[2][:, finish])
                 nc.sync.dma_start(out[:, finish], result[:, finish])
             fetch(1, first, count)
             fetch(2, first, count)
-            add(terms[:, 0, cols], terms[:, 0, cols], terms[:, 1, cols])
+            add(terms[0][:, cols], terms[0][:, cols], terms[1][:, cols])
             fetch(3, first, count)
-            add(terms[:, 2, cols], terms[:, 2, cols], ys[:, cols])
-            add(terms[:, 0, cols], terms[:, 0, cols], terms[:, 3, cols])
+            add(terms[2][:, cols], terms[2][:, cols], ys[:, cols])
+            add(terms[0][:, cols], terms[0][:, cols], terms[3][:, cols])
             finish = cols
-        add(result[:, finish], terms[:, 0, finish], terms[:, 2, finish])
+        add(result[:, finish], terms[0][:, finish], terms[2][:, finish])
         nc.sync.dma_start(out[:, finish], result[:, finish])

@@ -1,6 +1,7 @@
 from contextlib import ExitStack
 
 import concourse.mybir as mybir
+from concourse.masks import make_identity
 
 K, T, E, C, N = 2048, 1024, 16, 256, 128
 TOP = 4
@@ -22,9 +23,15 @@ P = 128
 PACK = 4
 PASSES = K // (P * PACK)
 PER_COL = 16
-PAIR = 2 * C
 BANK = 512
+WINDOW = 2 * T
 BIAS_BAY = 13
+CHUNKS = (range(0, 6), range(6, 12), range(12, 16))
+WORD_GATHERS = (
+    (0, 0, 0, 6), (1, 1, 0, 6), (2, 2, 0, 6), (3, 3, 0, 6),
+    (5, 0, 6, 12), (6, 1, 6, 12), (8, 2, 6, 12), (9, 3, 6, 12),
+    (11, 0, 12, 16), (12, 1, 12, 16), (14, 2, 12, 16), (14, 3, 12, 15), (15, 3, 15, 16),
+)
 
 
 def tile_moe_shr_lin_relu_kernel(
@@ -35,7 +42,7 @@ def tile_moe_shr_lin_relu_kernel(
         keep = ctx.enter_context(tc.tile_pool(name="keep", bufs=1))
         bays = ctx.enter_context(tc.tile_pool(name="bays", bufs=1))
         rounded = ctx.enter_context(tc.tile_pool(name="rounded", bufs=5))
-        packed = ctx.enter_context(tc.tile_pool(name="packed", bufs=10))
+        packed = ctx.enter_context(tc.tile_pool(name="packed", bufs=12))
         psum = ctx.enter_context(tc.psum_pool(name="psum", bufs=8))
 
         def in_bay(e, shape, dtype, name):
@@ -44,19 +51,24 @@ def tile_moe_shr_lin_relu_kernel(
         slot_tokens = keep.tile([P, S // PER_COL], U16, name="slot_tokens")
         nc.sync.dma_start(slot_tokens[:], offs)
 
-        tok_scales = keep.tile([P, T], U8, name="tok_scales", align_bytes=64)
-        nc.vector.memset(tok_scales[:].bitcast(I32), 0)
+        tok_scales = keep.tile([P, WINDOW], U8, name="tok_scales", align_bytes=64)
+        nc.vector.memset(tok_scales[:, 0:T].bitcast(I32), 0)
         for q in range(4):
             nc.sync.dma_start(
-                tok_scales[32 * q : 32 * q + 16, :].bitcast(I32),
+                tok_scales[32 * q : 32 * q + 16, 0:T].bitcast(I32),
                 x_scales[:, 4 * q : 4 * q + 4, :].bitcast(I32),
             )
 
-        tok_words = [keep.tile([P, T], I32, name="tok_words%d" % a, align_bytes=64) for a in range(PASSES)]
+        identity = keep.tile([P, P], F32, name="identity")
+        make_identity(nc, identity[:])
+
+        tok_words = keep.tile([P, (PASSES - 1) * T + WINDOW], I32, name="tok_words", align_bytes=64)
+        nc.vector.memset(tok_scales[:, T:WINDOW].bitcast(I32), 0)
+        nc.vector.memset(tok_words[:, PASSES * T :], 0)
         raw = {}
 
         def load_words(a):
-            nc.sync.dma_start(tok_words[a][:], x_words[a].rearrange("p t r -> p (t r)").bitcast(I32))
+            nc.sync.dma_start(tok_words[:, a * T : (a + 1) * T], x_words[a].rearrange("p t r -> p (t r)").bitcast(I32))
 
         def load_weight(e):
             raw[e] = in_bay(e, [P, PASSES, PACK * N], F32, "raw%d" % e)
@@ -65,12 +77,13 @@ def tile_moe_shr_lin_relu_kernel(
         load_weight(0)
         load_weight(1)
         load_words(0)
-        load_weight(2)
         load_words(1)
+        load_weight(2)
         load_words(2)
         load_weight(3)
+        load_weight(4)
         load_words(3)
-        for e in range(4, E + 1):
+        for e in range(5, E + 1):
             load_weight(e)
         token_slots = []
         for r, pos in enumerate((pos1, pos2, pos3, pos4)):
@@ -81,10 +94,11 @@ def tile_moe_shr_lin_relu_kernel(
             return lst[:, first // PER_COL : (first + count) // PER_COL]
 
         slot_scales = keep.tile([P, S], U8, name="slot_scales", align_bytes=64)
-        for g in range(E // 2):
+        for chunk in CHUNKS:
+            first, count = chunk.start * C, len(chunk) * C
             nc.vector.tensor_copy(
-                slot_scales[:, g * PAIR : (g + 1) * PAIR],
-                tok_scales[:].indirect(entries(slot_tokens, g * PAIR, PAIR)),
+                slot_scales[:, first : first + count],
+                tok_scales[:].indirect(entries(slot_tokens, first, count)),
             )
 
         grouped, w_words, w_scales = {}, {}, {}
@@ -116,29 +130,26 @@ def tile_moe_shr_lin_relu_kernel(
                 stop=(a == PASSES - 1),
             )
 
-        def gather_words(dst, a, first, count):
-            nc.vector.tensor_copy(dst, tok_words[a][:].bitcast(U32).indirect(entries(slot_tokens, first, count)))
-
         slot_words = {}
 
-        def gather_passes(e):
-            g, u = divmod(e, 2)
-            if e == BIAS_BAY:
+        def gather_words(bay):
+            jobs = [job[1:] for job in WORD_GATHERS if job[0] == bay]
+            if not jobs:
                 return
-            passes = range(PASSES) if e == BIAS_BAY - 1 else range(2 * u, 2 * u + 2)
-            held = in_bay(e, [P, len(passes), PAIR], U32, "slot_words%d" % e)
-            for i, a in enumerate(passes):
-                slot_words[g, a] = held[:, i, :]
-                if e == E - 1 and a == PASSES - 1:
-                    gather_words(held[:, i, 0:C], a, g * PAIR, C)
-                    gather_words(held[:, i, C:PAIR], a, g * PAIR + C, C)
-                else:
-                    gather_words(held[:, i, :], a, g * PAIR, PAIR)
+            held = in_bay(bay, [P, sum(hi - lo for a, lo, hi in jobs) * C], U32, "slot_words%d" % bay)
+            col = 0
+            for a, lo, hi in jobs:
+                count = (hi - lo) * C
+                window = tok_words[:, a * T : a * T + WINDOW].bitcast(U32)
+                nc.vector.tensor_copy(held[:, col : col + count], window.indirect(entries(slot_tokens, lo * C, count)))
+                for e in range(lo, hi):
+                    slot_words[e, a] = held[:, col + (e - lo) * C : col + (e - lo + 1) * C]
+                col += count
 
         for e in range(E):
             round_weight(e)
             quantize_weight(e)
-            gather_passes(e)
+            gather_words(e)
         round_weight(E)
 
         bias = in_bay(BIAS_BAY, [P, E + 1], F32, "bias")
@@ -148,19 +159,26 @@ def tile_moe_shr_lin_relu_kernel(
             nc.scalar.activation(dst, acc, RELU, bias=bias[:, e : e + 1])
 
         y = keep.tile([P, S], F32, name="y")
-        for g in range(E // 2):
-            accs = [psum.tile([P, BANK], F32, name="acc") for u in range(2)]
-            for a in range(PASSES):
-                for u in range(2):
-                    e = 2 * g + u
-                    multiply(
-                        accs[u][:, 0:C], e, a,
-                        slot_words[g, a][:, u * C : (u + 1) * C],
-                        slot_scales[4 * a : P, e * C : (e + 1) * C],
-                    )
-            for u in range(2):
-                e = 2 * g + u
-                activate(y[:, e * C : (e + 1) * C], accs[u][:, 0:C], e)
+        def routed(acc, e, a):
+            multiply(acc, e, a, slot_words[e, a], slot_scales[4 * a : P, e * C : (e + 1) * C])
+
+        for chunk in CHUNKS:
+            accs = {}
+            if chunk is CHUNKS[-1]:
+                waves = [chunk]
+                for e in chunk:
+                    accs[e] = psum.tile([P, C], F32, name="acc")[:]
+            else:
+                waves = [chunk[0::2], chunk[1::2]]
+                for e in waves[0]:
+                    bank = psum.tile([P, BANK], F32, name="acc")
+                    accs[e], accs[e + 1] = bank[:, 0:C], bank[:, C:BANK]
+            for wave in waves:
+                for a in range(PASSES):
+                    for e in wave:
+                        routed(accs[e], e, a)
+            for e in chunk:
+                activate(y[:, e * C : (e + 1) * C], accs[e], e)
 
         gates = []
         for h in range(2):
@@ -173,12 +191,13 @@ def tile_moe_shr_lin_relu_kernel(
             cols = slice(h * BANK, (h + 1) * BANK)
             acc = psum.tile([P, BANK], F32, name="acc")
             for a in range(PASSES):
-                multiply(acc[:], E, a, tok_words[a][:, cols], tok_scales[4 * a : P, cols])
+                multiply(acc[:], E, a, tok_words[:, a * T + h * BANK : a * T + (h + 1) * BANK], tok_scales[4 * a : P, cols])
             activate(ys[:, cols], acc[:], E)
 
         halves = [in_bay(2 + h, [P, 2, T], F32, "terms%d" % h) for h in range(2)]
         terms = [halves[r // 2][:, r % 2, :] for r in range(TOP)]
-        result = in_bay(5, [P, T], F32, "result")
+        result = in_bay(7, [P, T], F32, "result")
+        turned = in_bay(10, [P, T // P, N], F32, "turned")
 
         def fetch(r, first, count):
             nc.vector.tensor_tensor(
@@ -188,22 +207,35 @@ def tile_moe_shr_lin_relu_kernel(
                 MULT,
             )
 
-        def add(dst, lhs, rhs):
-            nc.vector.tensor_tensor(dst, lhs, rhs, ADD)
+        sums = [psum.tile([P, N], F32, name="acc") for blk in range(T // P)]
 
-        finish = None
-        for first, count in ((0, 640), (640, 384)):
+        def turn_and_add(src, blocks, start, stop):
+            for blk in blocks:
+                nc.tensor.matmul(
+                    sums[blk][:], src[:, blk * P : (blk + 1) * P], identity[:],
+                    start=start, stop=stop, is_transpose=True,
+                )
+
+        per_bank = BANK // P
+        fetch(0, 0, T)
+        turn_and_add(terms[0], range(T // P), True, False)
+        fetch(1, 0, T)
+        turn_and_add(terms[1], range(T // P), False, False)
+        turn_and_add(ys, range(T // P), False, False)
+        backs = []
+        for h in range(T // BANK):
+            blocks = range(h * per_bank, (h + 1) * per_bank)
+            fetch(2, h * BANK, BANK)
+            turn_and_add(terms[2], blocks, False, True)
+            for blk in blocks:
+                nc.scalar.copy(turned[:, blk, :], sums[blk][:])
+            backs.append(psum.tile([P, BANK], F32, name="acc"))
+            for i, blk in enumerate(blocks):
+                nc.tensor.transpose(backs[h][:, i * P : (i + 1) * P], turned[:, blk, :], identity[:])
+        for h in range(T // BANK):
+            fetch(3, h * BANK, BANK)
+        for first, count in ((0, 512), (512, 384), (896, 128)):
             cols = slice(first, first + count)
-            fetch(0, first, count)
-            if finish is not None:
-                add(result[:, finish], terms[0][:, finish], terms[2][:, finish])
-                nc.sync.dma_start(out[:, finish], result[:, finish])
-            fetch(1, first, count)
-            fetch(2, first, count)
-            add(terms[0][:, cols], terms[0][:, cols], terms[1][:, cols])
-            fetch(3, first, count)
-            add(terms[2][:, cols], terms[2][:, cols], ys[:, cols])
-            add(terms[0][:, cols], terms[0][:, cols], terms[3][:, cols])
-            finish = cols
-        add(result[:, finish], terms[0][:, finish], terms[2][:, finish])
-        nc.sync.dma_start(out[:, finish], result[:, finish])
+            h, within = divmod(first, BANK)
+            nc.vector.tensor_tensor(result[:, cols], backs[h][:, within : within + count], terms[3][:, cols], ADD)
+            nc.sync.dma_start(out[:, cols], result[:, cols])

@@ -25,12 +25,16 @@ PASSES = K // (P * PACK)
 PER_COL = 16
 BANK = 512
 WINDOW = 2 * T
-BIAS_BAY = 13
+EARLY_BIAS_BAY = 10
+LATE_BIAS_BAY = 14
+RAW_BAY = {E - 1: 3, E: E - 1}
+BIAS_AFTER = 6
+WORDS_AFTER = {2: 1, 4: 2, 5: 3}
 CHUNKS = (range(0, 6), range(6, 12), range(12, 16))
 WORD_GATHERS = (
-    (0, 0, 0, 6), (1, 1, 0, 6), (2, 2, 0, 6), (3, 3, 0, 6),
-    (5, 0, 6, 12), (6, 1, 6, 12), (8, 2, 6, 12), (9, 3, 6, 12),
-    (11, 0, 12, 16), (12, 1, 12, 16), (14, 2, 12, 16), (14, 3, 12, 15), (15, 3, 15, 16),
+    (E, 0, 0, 6), (0, 1, 0, 6), (1, 2, 0, 6), (2, 3, 0, 6),
+    (4, 0, 6, 12), (5, 1, 6, 12), (7, 2, 6, 12), (9, 3, 6, 12),
+    (11, 0, 12, 16), (12, 1, 12, 16), (15, 2, 12, 15), (15, 3, 12, 15), (15, 2, 15, 16), (15, 3, 15, 16),
 )
 
 
@@ -41,8 +45,8 @@ def tile_moe_shr_lin_relu_kernel(
     with ExitStack() as ctx:
         keep = ctx.enter_context(tc.tile_pool(name="keep", bufs=1))
         bays = ctx.enter_context(tc.tile_pool(name="bays", bufs=1))
-        rounded = ctx.enter_context(tc.tile_pool(name="rounded", bufs=5))
-        packed = ctx.enter_context(tc.tile_pool(name="packed", bufs=12))
+        rounded = ctx.enter_context(tc.tile_pool(name="rounded", bufs=6))
+        packed = ctx.enter_context(tc.tile_pool(name="packed", bufs=10))
         psum = ctx.enter_context(tc.psum_pool(name="psum", bufs=8))
 
         def in_bay(e, shape, dtype, name):
@@ -51,40 +55,40 @@ def tile_moe_shr_lin_relu_kernel(
         slot_tokens = keep.tile([P, S // PER_COL], U16, name="slot_tokens")
         nc.sync.dma_start(slot_tokens[:], offs)
 
+        tok_words = keep.tile([P, (PASSES - 1) * T + WINDOW], I32, name="tok_words", align_bytes=64)
         tok_scales = keep.tile([P, WINDOW], U8, name="tok_scales", align_bytes=64)
-        nc.vector.memset(tok_scales[:, 0:T].bitcast(I32), 0)
+        nc.vector.memset(tok_scales[:].bitcast(I32), 0)
+        nc.vector.memset(tok_words[:, PASSES * T :], 0)
+
+        def words_at(a):
+            return (PASSES - 1 - a) * T
+
+        def load_words(a):
+            nc.sync.dma_start(
+                tok_words[:, words_at(a) : words_at(a) + T], x_words[a].rearrange("p t r -> p (t r)").bitcast(I32)
+            )
+
+        raw = {}
+        all_bias = keep.tile([P, E + 1], F32, name="all_bias")
+
+        def load_weight(e):
+            raw[e] = in_bay(RAW_BAY.get(e, e), [P, PASSES, PACK * N], F32, "raw%d" % e)
+            nc.sync.dma_start(raw[e][:], w[e].rearrange("(a p j) n -> p a (j n)", a=PASSES, j=PACK))
+
+        load_words(0)
         for q in range(4):
             nc.sync.dma_start(
                 tok_scales[32 * q : 32 * q + 16, 0:T].bitcast(I32),
                 x_scales[:, 4 * q : 4 * q + 4, :].bitcast(I32),
             )
-
+        for e in list(range(E - 1)) + [E, E - 1]:
+            load_weight(e)
+            if e in WORDS_AFTER:
+                load_words(WORDS_AFTER[e])
+            if e == BIAS_AFTER:
+                nc.sync.dma_start(all_bias[:], b)
         identity = keep.tile([P, P], F32, name="identity")
         make_identity(nc, identity[:])
-
-        tok_words = keep.tile([P, (PASSES - 1) * T + WINDOW], I32, name="tok_words", align_bytes=64)
-        nc.vector.memset(tok_scales[:, T:WINDOW].bitcast(I32), 0)
-        nc.vector.memset(tok_words[:, PASSES * T :], 0)
-        raw = {}
-
-        def load_words(a):
-            nc.sync.dma_start(tok_words[:, a * T : (a + 1) * T], x_words[a].rearrange("p t r -> p (t r)").bitcast(I32))
-
-        def load_weight(e):
-            raw[e] = in_bay(e, [P, PASSES, PACK * N], F32, "raw%d" % e)
-            nc.sync.dma_start(raw[e][:], w[e].rearrange("(a p j) n -> p a (j n)", a=PASSES, j=PACK))
-
-        load_weight(0)
-        load_weight(1)
-        load_words(0)
-        load_words(1)
-        load_weight(2)
-        load_words(2)
-        load_weight(3)
-        load_weight(4)
-        load_words(3)
-        for e in range(5, E + 1):
-            load_weight(e)
         token_slots = []
         for r, pos in enumerate((pos1, pos2, pos3, pos4)):
             token_slots.append(keep.tile([P, T // PER_COL], U16, name="token_slots%d" % r))
@@ -92,14 +96,6 @@ def tile_moe_shr_lin_relu_kernel(
 
         def entries(lst, first, count):
             return lst[:, first // PER_COL : (first + count) // PER_COL]
-
-        slot_scales = keep.tile([P, S], U8, name="slot_scales", align_bytes=64)
-        for chunk in CHUNKS:
-            first, count = chunk.start * C, len(chunk) * C
-            nc.vector.tensor_copy(
-                slot_scales[:, first : first + count],
-                tok_scales[:].indirect(entries(slot_tokens, first, count)),
-            )
 
         grouped, w_words, w_scales = {}, {}, {}
 
@@ -111,8 +107,9 @@ def tile_moe_shr_lin_relu_kernel(
             )
 
         def quantize_weight(e):
-            w_words[e] = packed.tile([P, PASSES * N], U32, name="w_words", align_bytes=64)
-            w_scales[e] = packed.tile([P, PASSES * N], U8, name="w_scales", align_bytes=64)
+            pool = keep if e in (CHUNKS[-1].start, E) else packed
+            w_words[e] = pool.tile([P, PASSES * N], U32, name="w_words", align_bytes=64)
+            w_scales[e] = pool.tile([P, PASSES * N], U8, name="w_scales", align_bytes=64)
             nc.vector.quantize_mx(
                 out=w_words[e][:].bitcast(FP8X4),
                 scales=w_scales[e][:],
@@ -136,49 +133,64 @@ def tile_moe_shr_lin_relu_kernel(
             jobs = [job[1:] for job in WORD_GATHERS if job[0] == bay]
             if not jobs:
                 return
-            held = in_bay(bay, [P, sum(hi - lo for a, lo, hi in jobs) * C], U32, "slot_words%d" % bay)
+            held = in_bay(RAW_BAY.get(bay, bay) if bay < E else E, [P, sum(hi - lo for a, lo, hi in jobs) * C], U32, "slot_words%d" % bay)
             col = 0
             for a, lo, hi in jobs:
                 count = (hi - lo) * C
-                window = tok_words[:, a * T : a * T + WINDOW].bitcast(U32)
+                window = tok_words[:, words_at(a) : words_at(a) + WINDOW].bitcast(U32)
                 nc.vector.tensor_copy(held[:, col : col + count], window.indirect(entries(slot_tokens, lo * C, count)))
                 for e in range(lo, hi):
                     slot_words[e, a] = held[:, col + (e - lo) * C : col + (e - lo + 1) * C]
                 col += count
 
+        gather_words(E)
+        slot_scales = keep.tile([P, S], U8, name="slot_scales", align_bytes=64)
+        for chunk in CHUNKS:
+            first, count = chunk.start * C, len(chunk) * C
+            nc.vector.tensor_copy(
+                slot_scales[:, first : first + count],
+                tok_scales[:].indirect(entries(slot_tokens, first, count)),
+            )
+
+        y = keep.tile([P, S], F32, name="y")
+        bias = {}
+
+        def load_bias(bay, experts):
+            held = in_bay(bay, [P, len(experts)], F32, "bias%d" % bay)
+            nc.scalar.copy(held[:], all_bias[:, experts.start : experts.stop])
+            for e in experts:
+                bias[e] = held[:, e - experts.start : e - experts.start + 1]
+
+        def activate(dst, acc, e):
+            nc.scalar.activation(dst, acc, RELU, bias=bias[e])
+
+        def run_chunk(chunk):
+            accs = {}
+            if chunk is CHUNKS[-1]:
+                steps = [(e, a) for bay, a, lo, hi in WORD_GATHERS for e in range(lo, hi) if e in chunk]
+                for e in chunk:
+                    accs[e] = psum.tile([P, C], F32, name="acc")[:]
+            else:
+                steps = [(e, a) for wave in (chunk[0::2], chunk[1::2]) for a in range(PASSES) for e in wave]
+                for e in chunk[0::2]:
+                    bank = psum.tile([P, BANK], F32, name="acc")
+                    accs[e], accs[e + 1] = bank[:, 0:C], bank[:, C:BANK]
+            for e, a in steps:
+                multiply(accs[e], e, a, slot_words[e, a], slot_scales[4 * a : P, e * C : (e + 1) * C])
+            for e in chunk:
+                activate(y[:, e * C : (e + 1) * C], accs[e], e)
+
         for e in range(E):
             round_weight(e)
             quantize_weight(e)
             gather_words(e)
+            if e == EARLY_BIAS_BAY:
+                load_bias(e, CHUNKS[0])
+                run_chunk(CHUNKS[0])
         round_weight(E)
-
-        bias = in_bay(BIAS_BAY, [P, E + 1], F32, "bias")
-        nc.sync.dma_start(bias[:], b)
-
-        def activate(dst, acc, e):
-            nc.scalar.activation(dst, acc, RELU, bias=bias[:, e : e + 1])
-
-        y = keep.tile([P, S], F32, name="y")
-        def routed(acc, e, a):
-            multiply(acc, e, a, slot_words[e, a], slot_scales[4 * a : P, e * C : (e + 1) * C])
-
-        for chunk in CHUNKS:
-            accs = {}
-            if chunk is CHUNKS[-1]:
-                waves = [chunk]
-                for e in chunk:
-                    accs[e] = psum.tile([P, C], F32, name="acc")[:]
-            else:
-                waves = [chunk[0::2], chunk[1::2]]
-                for e in waves[0]:
-                    bank = psum.tile([P, BANK], F32, name="acc")
-                    accs[e], accs[e + 1] = bank[:, 0:C], bank[:, C:BANK]
-            for wave in waves:
-                for a in range(PASSES):
-                    for e in wave:
-                        routed(accs[e], e, a)
-            for e in chunk:
-                activate(y[:, e * C : (e + 1) * C], accs[e], e)
+        load_bias(LATE_BIAS_BAY, range(CHUNKS[1].start, E + 1))
+        for chunk in CHUNKS[1:]:
+            run_chunk(chunk)
 
         gates = []
         for h in range(2):
@@ -186,18 +198,18 @@ def tile_moe_shr_lin_relu_kernel(
             nc.sync.dma_start(gates[h][:], gate[2 * h : 2 * h + 2].rearrange("r p t -> p r t"))
 
         quantize_weight(E)
-        ys = in_bay(4, [P, T], F32, "ys")
+        ys = in_bay(6, [P, T], F32, "ys")
         for h in range(T // BANK):
             cols = slice(h * BANK, (h + 1) * BANK)
             acc = psum.tile([P, BANK], F32, name="acc")
             for a in range(PASSES):
-                multiply(acc[:], E, a, tok_words[:, a * T + h * BANK : a * T + (h + 1) * BANK], tok_scales[4 * a : P, cols])
+                multiply(acc[:], E, a, tok_words[:, words_at(a) + h * BANK : words_at(a) + (h + 1) * BANK], tok_scales[4 * a : P, cols])
             activate(ys[:, cols], acc[:], E)
 
-        halves = [in_bay(2 + h, [P, 2, T], F32, "terms%d" % h) for h in range(2)]
+        halves = [in_bay(2 + 2 * h, [P, 2, T], F32, "terms%d" % h) for h in range(2)]
         terms = [halves[r // 2][:, r % 2, :] for r in range(TOP)]
-        result = in_bay(7, [P, T], F32, "result")
-        turned = in_bay(10, [P, T // P, N], F32, "turned")
+        result = in_bay(8, [P, T], F32, "result")
+        turned = in_bay(5, [P, T // P, N], F32, "turned")
 
         def fetch(r, first, count):
             nc.vector.tensor_tensor(
@@ -232,10 +244,16 @@ def tile_moe_shr_lin_relu_kernel(
             backs.append(psum.tile([P, BANK], F32, name="acc"))
             for i, blk in enumerate(blocks):
                 nc.tensor.transpose(backs[h][:, i * P : (i + 1) * P], turned[:, blk, :], identity[:])
-        for h in range(T // BANK):
-            fetch(3, h * BANK, BANK)
-        for first, count in ((0, 512), (512, 384), (896, 128)):
+
+        def finish(first, count):
             cols = slice(first, first + count)
             h, within = divmod(first, BANK)
             nc.vector.tensor_tensor(result[:, cols], backs[h][:, within : within + count], terms[3][:, cols], ADD)
             nc.sync.dma_start(out[:, cols], result[:, cols])
+
+        pieces = ((0, 512), (512, 256), (768, 256))
+        fetch(3, *pieces[0])
+        for i, piece in enumerate(pieces):
+            if i + 1 < len(pieces):
+                fetch(3, *pieces[i + 1])
+            finish(*piece)

from contextlib import ExitStack

import concourse.mybir as mybir
from concourse.masks import make_identity

K, T, E, C, N = 2048, 1024, 16, 256, 128
TOP = 4
S = E * C
FLOPS = 2 * K * N * (S + T)

F32 = mybir.dt.float32
BF16 = mybir.dt.bfloat16
I32 = mybir.dt.int32
U32 = mybir.dt.uint32
U16 = mybir.dt.uint16
U8 = mybir.dt.uint8
FP8X4 = mybir.dt.float8_e4m3fn_x4
MULT = mybir.AluOpType.mult
ADD = mybir.AluOpType.add
RELU = mybir.ActivationFunctionType.Relu

P = 128
PACK = 4
PASSES = K // (P * PACK)
PER_COL = 16
BANK = 512
WINDOW = 2 * T
EARLY_BIAS_BAY = 10
LATE_BIAS_BAY = 14
RAW_BAY = {E - 1: 3, E: E - 1}
BIAS_AFTER = 6
WORDS_AFTER = {2: 1, 4: 2, 5: 3}
CHUNKS = (range(0, 6), range(6, 12), range(12, 16))
WORD_GATHERS = (
    (E, 0, 0, 6), (0, 1, 0, 6), (1, 2, 0, 6), (2, 3, 0, 6),
    (4, 0, 6, 12), (5, 1, 6, 12), (7, 2, 6, 12), (9, 3, 6, 12),
    (11, 0, 12, 16), (12, 1, 12, 16), (15, 2, 12, 15), (15, 3, 12, 15), (15, 2, 15, 16), (15, 3, 15, 16),
)


def tile_moe_shr_lin_relu_kernel(
    tc, x_words, x_scales, w, b, gate, offs, pos1, pos2, pos3, pos4, out
):
    nc = tc.nc
    with ExitStack() as ctx:
        keep = ctx.enter_context(tc.tile_pool(name="keep", bufs=1))
        bays = ctx.enter_context(tc.tile_pool(name="bays", bufs=1))
        rounded = ctx.enter_context(tc.tile_pool(name="rounded", bufs=6))
        packed = ctx.enter_context(tc.tile_pool(name="packed", bufs=10))
        psum = ctx.enter_context(tc.psum_pool(name="psum", bufs=8))

        def in_bay(e, shape, dtype, name):
            return bays.tile(shape, dtype, name=name, tag="bay%d" % e, align_bytes=64)

        slot_tokens = keep.tile([P, S // PER_COL], U16, name="slot_tokens")
        nc.sync.dma_start(slot_tokens[:], offs)

        tok_words = keep.tile([P, (PASSES - 1) * T + WINDOW], I32, name="tok_words", align_bytes=64)
        tok_scales = keep.tile([P, WINDOW], U8, name="tok_scales", align_bytes=64)
        nc.vector.memset(tok_scales[:].bitcast(I32), 0)
        nc.vector.memset(tok_words[:, PASSES * T :], 0)

        def words_at(a):
            return (PASSES - 1 - a) * T

        def load_words(a):
            nc.sync.dma_start(
                tok_words[:, words_at(a) : words_at(a) + T], x_words[a].rearrange("p t r -> p (t r)").bitcast(I32)
            )

        raw = {}
        all_bias = keep.tile([P, E + 1], F32, name="all_bias")

        def load_weight(e):
            raw[e] = in_bay(RAW_BAY.get(e, e), [P, PASSES, PACK * N], F32, "raw%d" % e)
            nc.sync.dma_start(raw[e][:], w[e].rearrange("(a p j) n -> p a (j n)", a=PASSES, j=PACK))

        load_words(0)
        for q in range(4):
            nc.sync.dma_start(
                tok_scales[32 * q : 32 * q + 16, 0:T].bitcast(I32),
                x_scales[:, 4 * q : 4 * q + 4, :].bitcast(I32),
            )
        for e in list(range(E - 1)) + [E, E - 1]:
            load_weight(e)
            if e in WORDS_AFTER:
                load_words(WORDS_AFTER[e])
            if e == BIAS_AFTER:
                nc.sync.dma_start(all_bias[:], b)
        identity = keep.tile([P, P], F32, name="identity")
        make_identity(nc, identity[:])
        token_slots = []
        for r, pos in enumerate((pos1, pos2, pos3, pos4)):
            token_slots.append(keep.tile([P, T // PER_COL], U16, name="token_slots%d" % r))
            nc.sync.dma_start(token_slots[r][:], pos)

        def entries(lst, first, count):
            return lst[:, first // PER_COL : (first + count) // PER_COL]

        grouped, w_words, w_scales = {}, {}, {}

        def round_weight(e):
            grouped[e] = rounded.tile([P, PASSES, N * PACK], BF16, name="grouped", align_bytes=64)
            nc.scalar.copy(
                grouped[e][:].rearrange("p a (c i j) -> p a c j i", i=4, j=PACK),
                raw[e][:].rearrange("p a (j c i) -> p a c j i", i=4, j=PACK),
            )

        def quantize_weight(e):
            pool = keep if e in (CHUNKS[-1].start, E) else packed
            w_words[e] = pool.tile([P, PASSES * N], U32, name="w_words", align_bytes=64)
            w_scales[e] = pool.tile([P, PASSES * N], U8, name="w_scales", align_bytes=64)
            nc.vector.quantize_mx(
                out=w_words[e][:].bitcast(FP8X4),
                scales=w_scales[e][:],
                in_=grouped[e][:].rearrange("p a x -> p (a x)"),
            )

        def multiply(acc, e, a, words, scales):
            nc.tensor.matmul_mx(
                out=acc,
                lhsT=w_words[e][:, a * N : (a + 1) * N].bitcast(FP8X4),
                lhsT_scale=w_scales[e][:, a * N : (a + 1) * N],
                rhs=words.bitcast(FP8X4),
                rhs_scale=scales,
                start=(a == 0),
                stop=(a == PASSES - 1),
            )

        slot_words = {}

        def gather_words(bay):
            jobs = [job[1:] for job in WORD_GATHERS if job[0] == bay]
            if not jobs:
                return
            held = in_bay(RAW_BAY.get(bay, bay) if bay < E else E, [P, sum(hi - lo for a, lo, hi in jobs) * C], U32, "slot_words%d" % bay)
            col = 0
            for a, lo, hi in jobs:
                count = (hi - lo) * C
                window = tok_words[:, words_at(a) : words_at(a) + WINDOW].bitcast(U32)
                nc.vector.tensor_copy(held[:, col : col + count], window.indirect(entries(slot_tokens, lo * C, count)))
                for e in range(lo, hi):
                    slot_words[e, a] = held[:, col + (e - lo) * C : col + (e - lo + 1) * C]
                col += count

        gather_words(E)
        slot_scales = keep.tile([P, S], U8, name="slot_scales", align_bytes=64)
        for chunk in CHUNKS:
            first, count = chunk.start * C, len(chunk) * C
            nc.vector.tensor_copy(
                slot_scales[:, first : first + count],
                tok_scales[:].indirect(entries(slot_tokens, first, count)),
            )

        y = keep.tile([P, S], F32, name="y")
        bias = {}

        def load_bias(bay, experts):
            held = in_bay(bay, [P, len(experts)], F32, "bias%d" % bay)
            nc.scalar.copy(held[:], all_bias[:, experts.start : experts.stop])
            for e in experts:
                bias[e] = held[:, e - experts.start : e - experts.start + 1]

        def activate(dst, acc, e):
            nc.scalar.activation(dst, acc, RELU, bias=bias[e])

        def run_chunk(chunk):
            accs = {}
            if chunk is CHUNKS[-1]:
                steps = [(e, a) for bay, a, lo, hi in WORD_GATHERS for e in range(lo, hi) if e in chunk]
                for e in chunk:
                    accs[e] = psum.tile([P, C], F32, name="acc")[:]
            else:
                steps = [(e, a) for wave in (chunk[0::2], chunk[1::2]) for a in range(PASSES) for e in wave]
                for e in chunk[0::2]:
                    bank = psum.tile([P, BANK], F32, name="acc")
                    accs[e], accs[e + 1] = bank[:, 0:C], bank[:, C:BANK]
            for e, a in steps:
                multiply(accs[e], e, a, slot_words[e, a], slot_scales[4 * a : P, e * C : (e + 1) * C])
            for e in chunk:
                activate(y[:, e * C : (e + 1) * C], accs[e], e)

        for e in range(E):
            round_weight(e)
            quantize_weight(e)
            gather_words(e)
            if e == EARLY_BIAS_BAY:
                load_bias(e, CHUNKS[0])
                run_chunk(CHUNKS[0])
        round_weight(E)
        load_bias(LATE_BIAS_BAY, range(CHUNKS[1].start, E + 1))
        for chunk in CHUNKS[1:]:
            run_chunk(chunk)

        gates = []
        for h in range(2):
            gates.append(in_bay(h, [P, 2, T], F32, "gates%d" % h))
            nc.sync.dma_start(gates[h][:], gate[2 * h : 2 * h + 2].rearrange("r p t -> p r t"))

        quantize_weight(E)
        ys = in_bay(6, [P, T], F32, "ys")
        for h in range(T // BANK):
            cols = slice(h * BANK, (h + 1) * BANK)
            acc = psum.tile([P, BANK], F32, name="acc")
            for a in range(PASSES):
                multiply(acc[:], E, a, tok_words[:, words_at(a) + h * BANK : words_at(a) + (h + 1) * BANK], tok_scales[4 * a : P, cols])
            activate(ys[:, cols], acc[:], E)

        halves = [in_bay(2 + 2 * h, [P, 2, T], F32, "terms%d" % h) for h in range(2)]
        terms = [halves[r // 2][:, r % 2, :] for r in range(TOP)]
        result = in_bay(8, [P, T], F32, "result")
        turned = in_bay(5, [P, T // P, N], F32, "turned")

        def fetch(r, first, count):
            nc.vector.tensor_tensor(
                terms[r][:, first : first + count],
                y[:].indirect(entries(token_slots[r], first, count)),
                gates[r // 2][:, r % 2, first : first + count],
                MULT,
            )

        sums = [psum.tile([P, N], F32, name="acc") for blk in range(T // P)]

        def turn_and_add(src, blocks, start, stop):
            for blk in blocks:
                nc.tensor.matmul(
                    sums[blk][:], src[:, blk * P : (blk + 1) * P], identity[:],
                    start=start, stop=stop, is_transpose=True,
                )

        per_bank = BANK // P
        fetch(0, 0, T)
        turn_and_add(terms[0], range(T // P), True, False)
        fetch(1, 0, T)
        turn_and_add(terms[1], range(T // P), False, False)
        turn_and_add(ys, range(T // P), False, False)
        backs = []
        for h in range(T // BANK):
            blocks = range(h * per_bank, (h + 1) * per_bank)
            fetch(2, h * BANK, BANK)
            turn_and_add(terms[2], blocks, False, True)
            for blk in blocks:
                nc.scalar.copy(turned[:, blk, :], sums[blk][:])
            backs.append(psum.tile([P, BANK], F32, name="acc"))
            for i, blk in enumerate(blocks):
                nc.tensor.transpose(backs[h][:, i * P : (i + 1) * P], turned[:, blk, :], identity[:])

        def finish(first, count):
            cols = slice(first, first + count)
            h, within = divmod(first, BANK)
            nc.vector.tensor_tensor(result[:, cols], backs[h][:, within : within + count], terms[3][:, cols], ADD)
            nc.sync.dma_start(out[:, cols], result[:, cols])

        pieces = ((0, 512), (512, 256), (768, 256))
        fetch(3, *pieces[0])
        for i, piece in enumerate(pieces):
            if i + 1 < len(pieces):
                fetch(3, *pieces[i + 1])
            finish(*piece)
